import numpy as np
import ml_dtypes


def mxq(x, axis, fmt="e4m3"):
    dtype, down = {"e4m3": (ml_dtypes.float8_e4m3fn, 7), "e5m2": (ml_dtypes.float8_e5m2, 14)}[fmt]
    v = np.moveaxis(np.asarray(x, np.float32).astype(ml_dtypes.bfloat16).astype(np.float64), axis, -1)
    blocks = v.reshape(v.shape[:-1] + (-1, 32))
    amax = np.abs(blocks).max(-1, keepdims=True)
    byte = np.maximum(np.where(amax > 0, np.frexp(amax)[1] - 1 + 127, 0) - down, 1)
    scale = np.exp2(byte - 127.0)
    codes = (blocks / scale).astype(np.float32).astype(dtype).astype(np.float64)
    return np.moveaxis((codes * scale).reshape(v.shape), -1, axis)


WIDE = False


def mx_kscale(k):
    if not WIDE:
        return np.ones(k)
    levels = np.array([10, -10, 5, -5, 0])
    if k % 512:
        return np.exp2(np.random.permutation(np.resize(levels, k // 32))).repeat(32)
    a = np.empty((k // 512, 16))
    for p in range(k // 512):
        a[p, :8] = np.random.permutation(np.resize(levels, 8))
        for g in range(8):
            far = levels[np.abs(levels - a[p, g]) >= 10]
            a[p, g + 8] = far[np.random.randint(len(far))]
    return np.exp2(a.ravel()).repeat(32)


def f64(x):
    return np.asarray(x).astype(np.float64)


def striped(idx):
    return np.tile(idx.reshape(-1, 16).T, (8, 1)).astype(np.uint16)


def unstriped(offs):
    return offs[:16].T.reshape(-1).astype(np.int64)


def striped8(idx):
    return np.concatenate([x.reshape(-1, 16).T for x in idx]).astype(np.uint16)


def runs(offs, k):
    lists = np.stack([offs[16 * r : 16 * r + 16].T.reshape(-1) for r in range(8)]).astype(np.int64)
    return lists[np.arange(k) % 512 // 64]


def pack_weight(w):
    k, n = w.shape
    w = f64(np.asarray(w, np.float32).astype(ml_dtypes.bfloat16)).reshape(k // 32, 32, n)
    amax = np.abs(w).max(1)
    byte = np.clip(np.where(amax > 0, np.frexp(amax)[1] - 1 + 127 - 7, 1), 1, 254)
    scaled = (w * np.exp2(127.0 - byte)[:, None, :]).reshape(k, n).astype(np.float32)
    words = np.ascontiguousarray(scaled.reshape(k // 512, 128, 4, n).transpose(0, 1, 3, 2)).astype(ml_dtypes.float8_e4m3fn).view(np.uint8)
    return words, np.ascontiguousarray(byte.astype(np.uint8).reshape(k // 512, 16, n))


def unpack_weight(words, scales):
    g, p, n, _ = words.shape
    vals = np.ascontiguousarray(words).view(ml_dtypes.float8_e4m3fn).astype(np.float64) * np.repeat(np.exp2(scales.astype(np.float64) - 127.0), 8, axis=1)[..., None]
    return vals.transpose(0, 1, 3, 2).reshape(g * 512, n)


K, T, S, N, H, U = 512, 2048, 256, 512, 512, 1024


def setup_inputs():
    n = np.random.standard_normal
    s = mx_kscale(K)[:, None]
    u = mx_kscale(H)
    packed_xT = pack_weight(n((K, T)) * s)
    return {
        "x_words": packed_xT[0],
        "x_scales": packed_xT[1],
        "w1": (n((K, H)) / np.sqrt(K) / s).astype(np.float32),
        "w2": (n((K, H)) / np.sqrt(K) / s).astype(np.float32),
        "gn": (np.random.uniform(0.5, 1.5, (H, 1)) * u[:, None]).astype(np.float32),
        "w3": (n((H, N)) / np.sqrt(H) / u[:, None]).astype(np.float32),
        "mem": n((N, U)).astype(np.float32),
        "offs": striped(np.random.permutation(T)[:S]),
        "two": striped(np.random.permutation(T)[:S]),
        "n1": striped8(np.stack([np.random.permutation(S) for _ in range(8)])),
        "n2": striped8(np.stack([np.random.permutation(S) for _ in range(8)])),
        "n3": striped(np.random.permutation(U)[:S]),
    }


def reference(x_words, x_scales, w1, w2, gn, w3, mem, offs, two, n1, n2, n3):
    xq = unpack_weight(x_words, x_scales)[:, unstriped(offs)]
    y = mxq(f64(w1), 0, "e4m3").T @ xq
    x_two = unpack_weight(x_words, x_scales)[:, unstriped(two)]
    d = mxq(f64(w2), 0, "e4m3").T @ x_two
    z = f64(gn) * (y[np.arange(H)[:, None], runs(n1, H)] - (np.tanh(d) * (d[np.arange(H)[:, None], runs(n2, H)])))
    h = mxq(f64(w3), 0, "e4m3").T @ mxq(z, 0, "e4m3")
    nw = np.maximum(h, 0.5 * f64(mem)[:, unstriped(n3)])
    out = f64(mem).copy()
    out[:, unstriped(n3)] = nw
    return out

@@ -1,0 +1,176 @@
+from contextlib import ExitStack
+
+import concourse.mybir as mybir
+
+K, T, S, H, N, U = 512, 2048, 256, 512, 512, 1024
+FLOPS = 2 * K * H * S * 2 + 2 * H * N * S
+
+F32 = mybir.dt.float32
+BF16 = mybir.dt.bfloat16
+I32 = mybir.dt.int32
+U32 = mybir.dt.uint32
+U16 = mybir.dt.uint16
+U8 = mybir.dt.uint8
+FP8X4 = mybir.dt.float8_e4m3fn_x4
+ALU = mybir.AluOpType
+ACT = mybir.ActivationFunctionType
+
+P = 128
+PACK = 4
+LIST_COLS = S // 16
+HALF = S // 2
+
+
+def tile_picked_twlsoftbpagex_none_p_kernel(
+    tc, x_words, x_scales, w1, w2, gn, w3, mem, offs, two, n1, n2, n3, out
+):
+    nc = tc.nc
+    with ExitStack() as ctx:
+        lists = ctx.enter_context(tc.tile_pool(name="lists", bufs=1))
+        sb = ctx.enter_context(tc.tile_pool(name="sb", bufs=1))
+        psum = ctx.enter_context(tc.psum_pool(name="psum", bufs=1))
+
+        def load_list(src, name):
+            tile = lists.tile([P, LIST_COLS], U16, name=name)
+            nc.sync.dma_start(tile[:], src)
+            return tile
+
+        def load_rows(src, name):
+            tile = sb.tile([P, PACK, src.shape[1]], F32, name=name)
+            nc.sync.dma_start(out=tile[:], in_=src.rearrange("(p j) c -> p j c", j=PACK))
+            return tile
+
+        scale_table = sb.tile([P, T], U8, name="scale_table")
+        nc.vector.memset(scale_table[:].bitcast(I32), 0)
+        def load_page(m):
+            page = sb.tile([P, U], F32, name="page%d" % m)
+            nc.sync.dma_start(out=page[:], in_=mem[m * P : (m + 1) * P, :])
+            return page
+
+        w2_raw = load_rows(w2, "w2_raw")
+        for q in range(4):
+            nc.sync.dma_start(
+                out=scale_table[32 * q : 32 * q + 4, :].bitcast(I32),
+                in_=x_scales[0, 4 * q : 4 * q + 4, :].bitcast(I32),
+            )
+        two_list = load_list(two, "two_list")
+        word_table = sb.tile([P, T], I32, name="word_table")
+        nc.sync.dma_start(out=word_table[:], in_=x_words[0].rearrange("p c r -> p (c r)").bitcast(I32))
+        offs_list = load_list(offs, "offs_list")
+        n2_list = load_list(n2, "n2_list")
+        gain = sb.tile([P, PACK], F32, name="gain")
+        nc.sync.dma_start(out=gain[:], in_=gn.rearrange("(p t) o -> p (t o)", t=PACK))
+        w1_raw = load_rows(w1, "w1_raw")
+        n1_list = load_list(n1, "n1_list")
+        n3_list = load_list(n3, "n3_list")
+        pages = [load_page(m) for m in range(N // P - 1)]
+        w3_raw = load_rows(w3, "w3_raw")
+        pages.append(load_page(N // P - 1))
+
+        def pick_words(entries, name):
+            words = sb.tile([P, S], U32, name=name, align_bytes=64)
+            nc.vector.tensor_copy(words[:], word_table[:].bitcast(U32).indirect(entries[:]))
+            return words
+
+        def pick_scales(entries, name):
+            scales = sb.tile([P, S], U8, name=name, align_bytes=64)
+            nc.vector.tensor_copy(scales[:], scale_table[:].indirect(entries[:]))
+            return scales
+
+        def quantise(grouped, name):
+            width = grouped.shape[1] // PACK
+            codes = sb.tile([P, width], U32, name=name + "_codes", align_bytes=64)
+            scales = sb.tile([P, width], U8, name=name + "_scales", align_bytes=64)
+            nc.vector.quantize_mx(out=codes[:].bitcast(FP8X4), scales=scales[:], in_=grouped)
+            return codes, scales
+
+        def product(acc, stationary, moving):
+            nc.tensor.matmul_mx(
+                out=acc,
+                lhsT=stationary[0][:].bitcast(FP8X4),
+                lhsT_scale=stationary[1][:],
+                rhs=moving[0][:].bitcast(FP8X4),
+                rhs_scale=moving[1][:],
+                start=True,
+                stop=True,
+            )
+
+        def deal_pair(copy, raw, pair, name):
+            grouped = sb.tile([P, 2, P * PACK], BF16, name=name, tag=name, align_bytes=64)
+            copy(
+                out=grouped[:].rearrange("p t (m j) -> p m j t", j=PACK),
+                in_=raw[:].rearrange("p j (m t) -> p m j t", t=PACK)[:, :, :, 2 * pair : 2 * pair + 2],
+            )
+            return [grouped[:, 0, :], grouped[:, 1, :]]
+
+        w2_grouped = deal_pair(nc.scalar.copy, w2_raw, 0, "w2_low") + deal_pair(nc.scalar.copy, w2_raw, 1, "w2_high")
+        two_scales = pick_scales(two_list, "two_scales")
+        w2_mx = [quantise(w2_grouped[t], "w2_%d" % t) for t in range(2)]
+        idx_scales = pick_scales(offs_list, "idx_scales")
+        x_two = (pick_words(two_list, "two_words"), two_scales)
+        w2_mx.extend(quantise(w2_grouped[t], "w2_%d" % t) for t in range(2, PACK))
+        d_rows = [sb.tile([P, 2 * S], F32, name="d_rows%d" % t, tag="d_rows%d" % t, align_bytes=64) for t in range(PACK)]
+        y_rows = [sb.tile([P, 2 * S], F32, name="y_rows%d" % t, tag="rows%d" % t, align_bytes=64) for t in range(PACK)]
+        for t in range(PACK):
+            acc = psum.tile([P, S], F32, name="d_acc%d" % t, tag="bank%d" % t)
+            product(acc[:], w2_mx[t], x_two)
+            nc.vector.tensor_copy(d_rows[t][:, :S], acc[:])
+            nc.scalar.activation(d_rows[t][:, S:], d_rows[t][:, :S], ACT.Tanh)
+            nc.scalar.activation(y_rows[t][:, S:], d_rows[t][:].indirect(n2_list[:]), ACT.Copy)
+
+        x_idx = (pick_words(offs_list, "idx_words"), idx_scales)
+        w1_grouped = deal_pair(nc.vector.tensor_copy, w1_raw, 0, "w1_low") + deal_pair(nc.vector.tensor_copy, w1_raw, 1, "w1_high")
+        y_accs = []
+        for t in range(PACK):
+            acc = psum.tile([P, S], F32, name="y_acc%d" % t, tag="bank%d" % (PACK + t))
+            product(acc[:], quantise(w1_grouped[t], "w1_%d" % t), x_idx)
+            y_accs.append(acc)
+        for t in range(PACK):
+            nc.vector.tensor_scalar(y_rows[t][:, :S], y_accs[t][:], gain[:, t : t + 1], None, ALU.mult)
+
+        y_picked = [sb.tile([P, PACK, HALF], F32, name="y_picked%d" % a, tag="y_picked%d" % a, align_bytes=64) for a in range(2)]
+        for a in range(2):
+            entries = n1_list[:, a * LIST_COLS // 2 : (a + 1) * LIST_COLS // 2]
+            for t in range(PACK):
+                nc.scalar.activation(y_picked[a][:, t, :], y_rows[t][:].indirect(entries), ACT.Copy)
+
+        gated = sb.tile([P, PACK, S], F32, name="gated", tag="w1_high", align_bytes=64)
+        for t in range(PACK):
+            nc.vector.scalar_tensor_tensor(gated[:, t, :], y_rows[t][:, S:], gain[:, t : t + 1], d_rows[t][:, S:], ALU.mult, ALU.mult)
+
+        def quantise_w3(m):
+            grouped = sb.tile([P, P * PACK], BF16, name="w3_grouped%d" % m, tag=("d_rows3", "y_picked1", "rows0", "rows1")[m], align_bytes=64)
+            nc.vector.tensor_copy(
+                out=grouped[:].rearrange("p (c i j) -> p c j i", i=4, j=PACK),
+                in_=w3_raw[:, :, m * P : (m + 1) * P].rearrange("p j (c i) -> p c j i", i=4),
+            )
+            return quantise(grouped[:], "w3_%d" % m)
+
+        w3_first = quantise_w3(0)
+
+        z_mx = []
+        for a in range(2):
+            z = sb.tile([P, HALF * PACK], BF16, name="z%d" % a, tag=("d_rows3", "y_picked0")[a], align_bytes=64)
+            nc.vector.tensor_tensor(
+                z[:].rearrange("p (c i t) -> p c t i", i=4, t=PACK),
+                y_picked[a][:].rearrange("p t (c i) -> p c t i", i=4),
+                gated[:, :, a * HALF : (a + 1) * HALF].rearrange("p t (c i) -> p c t i", i=4),
+                ALU.subtract,
+            )
+            z_mx.append(quantise(z[:], "z%d" % a))
+
+        held = []
+        for m in range(N // P):
+            old = sb.tile([P, S], F32, name="old%d" % m, tag="rows%d" % m, align_bytes=64)
+            nc.scalar.activation(old[:], pages[m][:].indirect(n3_list[:]), ACT.Copy)
+            held.append(old)
+
+        for m in range(N // P):
+            w3_mx = w3_first if m == 0 else quantise_w3(m)
+            acc = psum.tile([P, S], F32, name="h_acc%d" % m, tag="bank%d" % m)
+            for a in range(2):
+                product(acc[:, a * HALF : (a + 1) * HALF], w3_mx, z_mx[a])
+            new = sb.tile([P, S], F32, name="new%d" % m)
+            nc.vector.scalar_tensor_tensor(new[:], held[m][:], 0.5, acc[:], ALU.mult, ALU.max)
+            nc.scalar.activation(pages[m][:].indirect(n3_list[:]), new[:], ACT.Copy)
+            nc.sync.dma_start(out=out[m * P : (m + 1) * P, :], in_=pages[m][:])

@@ -19,6 +19,8 @@ P = 128
 PACK = 4
 LIST_COLS = S // 16
 HALF = S // 2
+SCALAR_COPIES = 2
+SCALAR_Y_COPIES = 1
 
 
 def tile_picked_twlsoftbpagex_none_p_kernel(
@@ -63,70 +65,79 @@ def tile_picked_twlsoftbpagex_none_p_kernel(
         w1_raw = load_rows(w1, "w1_raw")
         n1_list = load_list(n1, "n1_list")
         n3_list = load_list(n3, "n3_list")
-        pages = [load_page(m) for m in range(N // P - 1)]
+        pages = [load_page(m) for m in range(2)]
         w3_raw = load_rows(w3, "w3_raw")
-        pages.append(load_page(N // P - 1))
+        pages.extend(load_page(m) for m in range(2, N // P))
 
         def pick_words(entries, name):
             words = sb.tile([P, S], U32, name=name, align_bytes=64)
             nc.vector.tensor_copy(words[:], word_table[:].bitcast(U32).indirect(entries[:]))
-            return words
+            return words[:]
 
         def pick_scales(entries, name):
             scales = sb.tile([P, S], U8, name=name, align_bytes=64)
             nc.vector.tensor_copy(scales[:], scale_table[:].indirect(entries[:]))
-            return scales
+            return scales[:]
 
         def quantise(grouped, name):
             width = grouped.shape[1] // PACK
             codes = sb.tile([P, width], U32, name=name + "_codes", align_bytes=64)
             scales = sb.tile([P, width], U8, name=name + "_scales", align_bytes=64)
             nc.vector.quantize_mx(out=codes[:].bitcast(FP8X4), scales=scales[:], in_=grouped)
-            return codes, scales
+            return codes[:], scales[:]
+
+        def quantise_pair(grouped, name):
+            codes, scales = quantise(grouped, name)
+            return [(codes[:, u * P : (u + 1) * P], scales[:, u * P : (u + 1) * P]) for u in range(2)]
 
         def product(acc, stationary, moving):
             nc.tensor.matmul_mx(
                 out=acc,
-                lhsT=stationary[0][:].bitcast(FP8X4),
-                lhsT_scale=stationary[1][:],
-                rhs=moving[0][:].bitcast(FP8X4),
-                rhs_scale=moving[1][:],
+                lhsT=stationary[0].bitcast(FP8X4),
+                lhsT_scale=stationary[1],
+                rhs=moving[0].bitcast(FP8X4),
+                rhs_scale=moving[1],
                 start=True,
                 stop=True,
             )
 
         def deal_pair(copy, raw, pair, name):
-            grouped = sb.tile([P, 2, P * PACK], BF16, name=name, tag=name, align_bytes=64)
+            grouped = sb.tile([P, 2 * P * PACK], BF16, name=name, tag=name, align_bytes=64)
             copy(
-                out=grouped[:].rearrange("p t (m j) -> p m j t", j=PACK),
+                out=grouped[:].rearrange("p (t m j) -> p m j t", t=2, j=PACK),
                 in_=raw[:].rearrange("p j (m t) -> p m j t", t=PACK)[:, :, :, 2 * pair : 2 * pair + 2],
             )
-            return [grouped[:, 0, :], grouped[:, 1, :]]
+            return grouped[:]
 
-        w2_grouped = deal_pair(nc.scalar.copy, w2_raw, 0, "w2_low") + deal_pair(nc.scalar.copy, w2_raw, 1, "w2_high")
+        w2_grouped = [deal_pair(nc.scalar.copy, w2_raw, pair, "w2_pair%d" % pair) for pair in range(2)]
         two_scales = pick_scales(two_list, "two_scales")
-        w2_mx = [quantise(w2_grouped[t], "w2_%d" % t) for t in range(2)]
+        w2_mx = quantise_pair(w2_grouped[0], "w2_low")
         idx_scales = pick_scales(offs_list, "idx_scales")
         x_two = (pick_words(two_list, "two_words"), two_scales)
-        w2_mx.extend(quantise(w2_grouped[t], "w2_%d" % t) for t in range(2, PACK))
+        w2_mx.extend(quantise_pair(w2_grouped[1], "w2_high"))
         d_rows = [sb.tile([P, 2 * S], F32, name="d_rows%d" % t, tag="d_rows%d" % t, align_bytes=64) for t in range(PACK)]
         y_rows = [sb.tile([P, 2 * S], F32, name="y_rows%d" % t, tag="rows%d" % t, align_bytes=64) for t in range(PACK)]
         for t in range(PACK):
             acc = psum.tile([P, S], F32, name="d_acc%d" % t, tag="bank%d" % t)
             product(acc[:], w2_mx[t], x_two)
-            nc.vector.tensor_copy(d_rows[t][:, :S], acc[:])
-            nc.scalar.activation(d_rows[t][:, S:], d_rows[t][:, :S], ACT.Tanh)
+            nc.scalar.activation(d_rows[t][:, S:], acc[:], ACT.Tanh)
+            if t >= PACK - SCALAR_COPIES:
+                nc.scalar.activation(d_rows[t][:, :S], acc[:], ACT.Copy, scale=gain[:, t : t + 1])
+            else:
+                nc.vector.tensor_scalar(d_rows[t][:, :S], acc[:], gain[:, t : t + 1], None, ALU.mult)
+        for t in range(PACK):
             nc.scalar.activation(y_rows[t][:, S:], d_rows[t][:].indirect(n2_list[:]), ACT.Copy)
 
         x_idx = (pick_words(offs_list, "idx_words"), idx_scales)
-        w1_grouped = deal_pair(nc.vector.tensor_copy, w1_raw, 0, "w1_low") + deal_pair(nc.vector.tensor_copy, w1_raw, 1, "w1_high")
-        y_accs = []
+        w1_grouped = [deal_pair(nc.vector.tensor_copy, w1_raw, pair, "w1_pair%d" % pair) for pair in range(2)]
+        w1_mx = quantise_pair(w1_grouped[0], "w1_low") + quantise_pair(w1_grouped[1], "w1_high")
         for t in range(PACK):
             acc = psum.tile([P, S], F32, name="y_acc%d" % t, tag="bank%d" % (PACK + t))
-            product(acc[:], quantise(w1_grouped[t], "w1_%d" % t), x_idx)
-            y_accs.append(acc)
-        for t in range(PACK):
-            nc.vector.tensor_scalar(y_rows[t][:, :S], y_accs[t][:], gain[:, t : t + 1], None, ALU.mult)
+            product(acc[:], w1_mx[t], x_idx)
+            if t >= PACK - SCALAR_Y_COPIES:
+                nc.scalar.activation(y_rows[t][:, :S], acc[:], ACT.Copy, scale=gain[:, t : t + 1])
+            else:
+                nc.vector.tensor_scalar(y_rows[t][:, :S], acc[:], gain[:, t : t + 1], None, ALU.mult)
 
         y_picked = [sb.tile([P, PACK, HALF], F32, name="y_picked%d" % a, tag="y_picked%d" % a, align_bytes=64) for a in range(2)]
         for a in range(2):
@@ -134,30 +145,32 @@ def tile_picked_twlsoftbpagex_none_p_kernel(
             for t in range(PACK):
                 nc.scalar.activation(y_picked[a][:, t, :], y_rows[t][:].indirect(entries), ACT.Copy)
 
-        gated = sb.tile([P, PACK, S], F32, name="gated", tag="w1_high", align_bytes=64)
-        for t in range(PACK):
-            nc.vector.scalar_tensor_tensor(gated[:, t, :], y_rows[t][:, S:], gain[:, t : t + 1], d_rows[t][:, S:], ALU.mult, ALU.mult)
-
-        def quantise_w3(m):
-            grouped = sb.tile([P, P * PACK], BF16, name="w3_grouped%d" % m, tag=("d_rows3", "y_picked1", "rows0", "rows1")[m], align_bytes=64)
+        def group_w3(m):
+            grouped = sb.tile([P, P * PACK], BF16, name="w3_grouped%d" % m, tag=("d_rows2", "y_picked0", "rows0", "rows1")[m], align_bytes=64)
             nc.vector.tensor_copy(
-                out=grouped[:].rearrange("p (c i j) -> p c j i", i=4, j=PACK),
-                in_=w3_raw[:, :, m * P : (m + 1) * P].rearrange("p j (c i) -> p c j i", i=4),
+                out=grouped[:].rearrange("p (c i j) -> p c j i", i=2, j=PACK),
+                in_=w3_raw[:, :, m * P : (m + 1) * P].rearrange("p j (c i) -> p c j i", i=2),
             )
-            return quantise(grouped[:], "w3_%d" % m)
+            return grouped[:]
 
-        w3_first = quantise_w3(0)
+        gated = sb.tile([P, PACK, S], F32, name="gated", tag="w1_pair1", align_bytes=64)
+        for t in range(PACK):
+            if t == PACK - 1:
+                w3_first_grouped = group_w3(0)
+            nc.vector.tensor_tensor(gated[:, t, :], y_rows[t][:, S:], d_rows[t][:, S:], ALU.mult)
+        w3_first = quantise(w3_first_grouped, "w3_0")
 
-        z_mx = []
+        z_grouped = []
         for a in range(2):
-            z = sb.tile([P, HALF * PACK], BF16, name="z%d" % a, tag=("d_rows3", "y_picked0")[a], align_bytes=64)
+            z = sb.tile([P, HALF * PACK], BF16, name="z%d" % a, tag=("d_rows2", "y_picked0")[a], align_bytes=64)
             nc.vector.tensor_tensor(
-                z[:].rearrange("p (c i t) -> p c t i", i=4, t=PACK),
-                y_picked[a][:].rearrange("p t (c i) -> p c t i", i=4),
-                gated[:, :, a * HALF : (a + 1) * HALF].rearrange("p t (c i) -> p c t i", i=4),
+                z[:].rearrange("p (c i t) -> p c t i", i=2, t=PACK),
+                y_picked[a][:].rearrange("p t (c i) -> p c t i", i=2),
+                gated[:, :, a * HALF : (a + 1) * HALF].rearrange("p t (c i) -> p c t i", i=2),
                 ALU.subtract,
             )
-            z_mx.append(quantise(z[:], "z%d" % a))
+            z_grouped.append(z[:])
+        z_mx = [quantise(z_grouped[a], "z%d" % a) for a in range(2)]
 
         held = []
         for m in range(N // P):
@@ -166,7 +179,7 @@ def tile_picked_twlsoftbpagex_none_p_kernel(
             held.append(old)
 
         for m in range(N // P):
-            w3_mx = w3_first if m == 0 else quantise_w3(m)
+            w3_mx = w3_first if m == 0 else quantise(group_w3(m), "w3_%d" % m)
             acc = psum.tile([P, S], F32, name="h_acc%d" % m, tag="bank%d" % m)
             for a in range(2):
                 product(acc[:, a * HALF : (a + 1) * HALF], w3_mx, z_mx[a])

from contextlib import ExitStack

import concourse.mybir as mybir

K, T, S, H, N, U = 512, 2048, 256, 512, 512, 1024
FLOPS = 2 * K * H * S * 2 + 2 * H * N * S

F32 = mybir.dt.float32
BF16 = mybir.dt.bfloat16
I32 = mybir.dt.int32
U32 = mybir.dt.uint32
U16 = mybir.dt.uint16
U8 = mybir.dt.uint8
FP8X4 = mybir.dt.float8_e4m3fn_x4
ALU = mybir.AluOpType
ACT = mybir.ActivationFunctionType

P = 128
PACK = 4
LIST_COLS = S // 16
HALF = S // 2
SCALAR_COPIES = 2
SCALAR_Y_COPIES = 1


def tile_picked_twlsoftbpagex_none_p_kernel(
    tc, x_words, x_scales, w1, w2, gn, w3, mem, offs, two, n1, n2, n3, out
):
    nc = tc.nc
    with ExitStack() as ctx:
        lists = ctx.enter_context(tc.tile_pool(name="lists", bufs=1))
        sb = ctx.enter_context(tc.tile_pool(name="sb", bufs=1))
        psum = ctx.enter_context(tc.psum_pool(name="psum", bufs=1))

        def load_list(src, name):
            tile = lists.tile([P, LIST_COLS], U16, name=name)
            nc.sync.dma_start(tile[:], src)
            return tile

        def load_rows(src, name):
            tile = sb.tile([P, PACK, src.shape[1]], F32, name=name)
            nc.sync.dma_start(out=tile[:], in_=src.rearrange("(p j) c -> p j c", j=PACK))
            return tile

        scale_table = sb.tile([P, T], U8, name="scale_table")
        nc.vector.memset(scale_table[:].bitcast(I32), 0)
        def load_page(m):
            page = sb.tile([P, U], F32, name="page%d" % m)
            nc.sync.dma_start(out=page[:], in_=mem[m * P : (m + 1) * P, :])
            return page

        w2_raw = load_rows(w2, "w2_raw")
        for q in range(4):
            nc.sync.dma_start(
                out=scale_table[32 * q : 32 * q + 4, :].bitcast(I32),
                in_=x_scales[0, 4 * q : 4 * q + 4, :].bitcast(I32),
            )
        two_list = load_list(two, "two_list")
        word_table = sb.tile([P, T], I32, name="word_table")
        nc.sync.dma_start(out=word_table[:], in_=x_words[0].rearrange("p c r -> p (c r)").bitcast(I32))
        offs_list = load_list(offs, "offs_list")
        n2_list = load_list(n2, "n2_list")
        gain = sb.tile([P, PACK], F32, name="gain")
        nc.sync.dma_start(out=gain[:], in_=gn.rearrange("(p t) o -> p (t o)", t=PACK))
        w1_raw = load_rows(w1, "w1_raw")
        n1_list = load_list(n1, "n1_list")
        n3_list = load_list(n3, "n3_list")
        pages = [load_page(m) for m in range(2)]
        w3_raw = load_rows(w3, "w3_raw")
        pages.extend(load_page(m) for m in range(2, N // P))

        def pick_words(entries, name):
            words = sb.tile([P, S], U32, name=name, align_bytes=64)
            nc.vector.tensor_copy(words[:], word_table[:].bitcast(U32).indirect(entries[:]))
            return words[:]

        def pick_scales(entries, name):
            scales = sb.tile([P, S], U8, name=name, align_bytes=64)
            nc.vector.tensor_copy(scales[:], scale_table[:].indirect(entries[:]))
            return scales[:]

        def quantise(grouped, name):
            width = grouped.shape[1] // PACK
            codes = sb.tile([P, width], U32, name=name + "_codes", align_bytes=64)
            scales = sb.tile([P, width], U8, name=name + "_scales", align_bytes=64)
            nc.vector.quantize_mx(out=codes[:].bitcast(FP8X4), scales=scales[:], in_=grouped)
            return codes[:], scales[:]

        def quantise_pair(grouped, name):
            codes, scales = quantise(grouped, name)
            return [(codes[:, u * P : (u + 1) * P], scales[:, u * P : (u + 1) * P]) for u in range(2)]

        def product(acc, stationary, moving):
            nc.tensor.matmul_mx(
                out=acc,
                lhsT=stationary[0].bitcast(FP8X4),
                lhsT_scale=stationary[1],
                rhs=moving[0].bitcast(FP8X4),
                rhs_scale=moving[1],
                start=True,
                stop=True,
            )

        def deal_pair(copy, raw, pair, name):
            grouped = sb.tile([P, 2 * P * PACK], BF16, name=name, tag=name, align_bytes=64)
            copy(
                out=grouped[:].rearrange("p (t m j) -> p m j t", t=2, j=PACK),
                in_=raw[:].rearrange("p j (m t) -> p m j t", t=PACK)[:, :, :, 2 * pair : 2 * pair + 2],
            )
            return grouped[:]

        w2_grouped = [deal_pair(nc.scalar.copy, w2_raw, pair, "w2_pair%d" % pair) for pair in range(2)]
        two_scales = pick_scales(two_list, "two_scales")
        w2_mx = quantise_pair(w2_grouped[0], "w2_low")
        idx_scales = pick_scales(offs_list, "idx_scales")
        x_two = (pick_words(two_list, "two_words"), two_scales)
        w2_mx.extend(quantise_pair(w2_grouped[1], "w2_high"))
        d_rows = [sb.tile([P, 2 * S], F32, name="d_rows%d" % t, tag="d_rows%d" % t, align_bytes=64) for t in range(PACK)]
        y_rows = [sb.tile([P, 2 * S], F32, name="y_rows%d" % t, tag="rows%d" % t, align_bytes=64) for t in range(PACK)]
        for t in range(PACK):
            acc = psum.tile([P, S], F32, name="d_acc%d" % t, tag="bank%d" % t)
            product(acc[:], w2_mx[t], x_two)
            nc.scalar.activation(d_rows[t][:, S:], acc[:], ACT.Tanh)
            if t >= PACK - SCALAR_COPIES:
                nc.scalar.activation(d_rows[t][:, :S], acc[:], ACT.Copy, scale=gain[:, t : t + 1])
            else:
                nc.vector.tensor_scalar(d_rows[t][:, :S], acc[:], gain[:, t : t + 1], None, ALU.mult)
        for t in range(PACK):
            nc.scalar.activation(y_rows[t][:, S:], d_rows[t][:].indirect(n2_list[:]), ACT.Copy)

        x_idx = (pick_words(offs_list, "idx_words"), idx_scales)
        w1_grouped = [deal_pair(nc.vector.tensor_copy, w1_raw, pair, "w1_pair%d" % pair) for pair in range(2)]
        w1_mx = quantise_pair(w1_grouped[0], "w1_low") + quantise_pair(w1_grouped[1], "w1_high")
        for t in range(PACK):
            acc = psum.tile([P, S], F32, name="y_acc%d" % t, tag="bank%d" % (PACK + t))
            product(acc[:], w1_mx[t], x_idx)
            if t >= PACK - SCALAR_Y_COPIES:
                nc.scalar.activation(y_rows[t][:, :S], acc[:], ACT.Copy, scale=gain[:, t : t + 1])
            else:
                nc.vector.tensor_scalar(y_rows[t][:, :S], acc[:], gain[:, t : t + 1], None, ALU.mult)

        y_picked = [sb.tile([P, PACK, HALF], F32, name="y_picked%d" % a, tag="y_picked%d" % a, align_bytes=64) for a in range(2)]
        for a in range(2):
            entries = n1_list[:, a * LIST_COLS // 2 : (a + 1) * LIST_COLS // 2]
            for t in range(PACK):
                nc.scalar.activation(y_picked[a][:, t, :], y_rows[t][:].indirect(entries), ACT.Copy)

        def group_w3(m):
            grouped = sb.tile([P, P * PACK], BF16, name="w3_grouped%d" % m, tag=("d_rows2", "y_picked0", "rows0", "rows1")[m], align_bytes=64)
            nc.vector.tensor_copy(
                out=grouped[:].rearrange("p (c i j) -> p c j i", i=2, j=PACK),
                in_=w3_raw[:, :, m * P : (m + 1) * P].rearrange("p j (c i) -> p c j i", i=2),
            )
            return grouped[:]

        gated = sb.tile([P, PACK, S], F32, name="gated", tag="w1_pair1", align_bytes=64)
        for t in range(PACK):
            if t == PACK - 1:
                w3_first_grouped = group_w3(0)
            nc.vector.tensor_tensor(gated[:, t, :], y_rows[t][:, S:], d_rows[t][:, S:], ALU.mult)
        w3_first = quantise(w3_first_grouped, "w3_0")

        z_grouped = []
        for a in range(2):
            z = sb.tile([P, HALF * PACK], BF16, name="z%d" % a, tag=("d_rows2", "y_picked0")[a], align_bytes=64)
            nc.vector.tensor_tensor(
                z[:].rearrange("p (c i t) -> p c t i", i=2, t=PACK),
                y_picked[a][:].rearrange("p t (c i) -> p c t i", i=2),
                gated[:, :, a * HALF : (a + 1) * HALF].rearrange("p t (c i) -> p c t i", i=2),
                ALU.subtract,
            )
            z_grouped.append(z[:])
        z_mx = [quantise(z_grouped[a], "z%d" % a) for a in range(2)]

        held = []
        for m in range(N // P):
            old = sb.tile([P, S], F32, name="old%d" % m, tag="rows%d" % m, align_bytes=64)
            nc.scalar.activation(old[:], pages[m][:].indirect(n3_list[:]), ACT.Copy)
            held.append(old)

        for m in range(N // P):
            w3_mx = w3_first if m == 0 else quantise(group_w3(m), "w3_%d" % m)
            acc = psum.tile([P, S], F32, name="h_acc%d" % m, tag="bank%d" % m)
            for a in range(2):
                product(acc[:, a * HALF : (a + 1) * HALF], w3_mx, z_mx[a])
            new = sb.tile([P, S], F32, name="new%d" % m)
            nc.vector.scalar_tensor_tensor(new[:], held[m][:], 0.5, acc[:], ALU.mult, ALU.max)
            nc.scalar.activation(pages[m][:].indirect(n3_list[:]), new[:], ACT.Copy)
            nc.sync.dma_start(out=out[m * P : (m + 1) * P, :], in_=pages[m][:])
